import numpy as np
import ml_dtypes


def mxq(x, axis, fmt="e4m3"):
    dtype, down = {"e4m3": (ml_dtypes.float8_e4m3fn, 7), "e5m2": (ml_dtypes.float8_e5m2, 14)}[fmt]
    v = np.moveaxis(np.asarray(x, np.float32).astype(ml_dtypes.bfloat16).astype(np.float64), axis, -1)
    blocks = v.reshape(v.shape[:-1] + (-1, 32))
    amax = np.abs(blocks).max(-1, keepdims=True)
    byte = np.maximum(np.where(amax > 0, np.frexp(amax)[1] - 1 + 127, 0) - down, 1)
    scale = np.exp2(byte - 127.0)
    codes = (blocks / scale).astype(np.float32).astype(dtype).astype(np.float64)
    return np.moveaxis((codes * scale).reshape(v.shape), -1, axis)


WIDE = False


def mx_kscale(k):
    if not WIDE:
        return np.ones(k)
    levels = np.array([10, -10, 5, -5, 0])
    if k % 512:
        return np.exp2(np.random.permutation(np.resize(levels, k // 32))).repeat(32)
    a = np.empty((k // 512, 16))
    for p in range(k // 512):
        a[p, :8] = np.random.permutation(np.resize(levels, 8))
        for g in range(8):
            far = levels[np.abs(levels - a[p, g]) >= 10]
            a[p, g + 8] = far[np.random.randint(len(far))]
    return np.exp2(a.ravel()).repeat(32)


def f64(x):
    return np.asarray(x).astype(np.float64)


def striped(idx):
    return np.tile(np.asarray(idx).reshape(-1, 16).T, (8, 1)).astype(np.uint16)


def unstriped(offs):
    return offs[:16].T.reshape(-1).astype(np.int64)


E2M1 = np.array([0.0, 0.5, 1.0, 1.5, 2.0, 3.0, 4.0, 6.0, -0.0, -0.5, -1.0, -1.5, -2.0, -3.0, -4.0, -6.0])


def pack_weight(w, fmt):
    k, n = w.shape
    w = f64(np.asarray(w, np.float32).astype(ml_dtypes.bfloat16)).reshape(k // 32, 32, n)
    amax = np.abs(w).max(1)
    if fmt == "e4m3":
        byte = np.frexp(amax)[1] - 1 + 127 - 7
    else:
        mant, ex = np.frexp(amax / 6.0)
        byte = np.where(mant > 0.5, ex, ex - 1) + 127
    byte = np.clip(np.where(amax > 0, byte, 1), 1, 254)
    scaled = (w * np.exp2(127.0 - byte)[:, None, :]).reshape(k, n).astype(np.float32)
    by_word = np.ascontiguousarray(scaled.reshape(k // 512, 128, 4, n).transpose(0, 1, 3, 2))
    if fmt == "e4m3":
        words = by_word.astype(ml_dtypes.float8_e4m3fn).view(np.uint8)
    else:
        c = by_word.astype(ml_dtypes.float4_e2m1fn).view(np.uint8) & 0xF
        words = (c[..., 0::2] | (c[..., 1::2] << 4)).reshape(k // 512, 128, 2 * n)
    return np.ascontiguousarray(words), np.ascontiguousarray(byte.astype(np.uint8).reshape(k // 512, 16, n))


def unpack_weight(words, scales, fmt):
    g, _, n = scales.shape
    words = np.ascontiguousarray(words).reshape(g, 128, n, -1)
    if fmt == "e4m3":
        vals = words.view(ml_dtypes.float8_e4m3fn).astype(np.float64)
    else:
        nib = np.empty((g, 128, n, 4), np.uint8)
        nib[..., 0::2] = words & 0xF
        nib[..., 1::2] = words >> 4
        vals = E2M1[nib]
    vals = vals * np.repeat(np.exp2(scales.astype(np.float64) - 127.0), 8, axis=1)[..., None]
    return vals.transpose(0, 1, 3, 2).reshape(g * 512, n)


D, K, R, T, I, Q = 512, 512, 512, 2048, 512, 128


def setup_inputs():
    n = np.random.standard_normal
    idx = np.random.permutation(T)[:I]
    fd = mx_kscale(D)
    fk = mx_kscale(K)
    fi = mx_kscale(I)
    keysp = pack_weight(n((D, T)) / fd[:, None], "e2m1")
    tabp = pack_weight(n((K, T)) / fk[:, None], "e2m1")
    return {
        "query": (n((D, Q)) * 0.7 / np.sqrt(D) * fd[:, None]).astype(np.float32),
        "keys_words": keysp[0],
        "keys_scales": keysp[1],
        "tab_words": tabp[0],
        "tab_scales": tabp[1],
        "w1": (n((K, R)) * 1 / np.sqrt(K) * fk[:, None]).astype(np.float32),
        "gain": (np.random.uniform(0.5, 2.0, (R, 1))).astype(np.float32),
        "os": (np.random.uniform(4.0, 16.0, (1, I)) * fi).astype(np.float32),
        "vs": (np.random.uniform(0.5, 2.0, (1, I)) / fi).astype(np.float32),
        "offs": striped(idx),
    }


def reference(query, keys_words, keys_scales, tab_words, tab_scales, w1, gain, os, vs, offs):
    idx = unstriped(offs)
    keysu = unpack_weight(keys_words, keys_scales, "e2m1")
    tabu = unpack_weight(tab_words, tab_scales, "e2m1")
    queryq = mxq(f64(query), 0, "e4m3")
    keysidxg = keysu[:, idx]
    a = queryq.T @ keysidxg
    p = np.exp(a - np.max(a, axis=1, keepdims=True))
    z = np.sum(p, axis=1, keepdims=True)
    w = p / z
    w1q = mxq(f64(w1), 0, "e4m3")
    tabidxg = tabu[:, idx]
    zh = w1q.T @ tabidxg
    ht = np.tanh(zh)
    hv = ht * f64(gain)
    wo1 = w * f64(os)
    wt1 = wo1.T
    hw = hv * f64(vs)
    ht1 = hw.T
    wt1q = mxq(wt1, 0, "e4m3")
    ht1q = mxq(ht1, 0, "e4m3")
    o = wt1q.T @ ht1q
    return o

@@ -1,0 +1,178 @@
+from contextlib import ExitStack
+
+import concourse.mybir as mybir
+from concourse.masks import make_identity
+
+D, K, R, T, I, Q = 512, 512, 512, 2048, 512, 128
+FLOPS = 2 * (D * Q * I + K * R * I + I * Q * R)
+
+F32 = mybir.dt.float32
+BF16 = mybir.dt.bfloat16
+I32 = mybir.dt.int32
+U32 = mybir.dt.uint32
+U16 = mybir.dt.uint16
+U8 = mybir.dt.uint8
+FP8X4 = mybir.dt.float8_e4m3fn_x4
+FP4X4 = mybir.dt.float4_e2m1fn_x4
+ACT = mybir.ActivationFunctionType
+ALU = mybir.AluOpType
+
+P = 128
+PACK = 4
+CHUNKS = R // P
+W1_PARTS = 2
+W1_COLS = R // W1_PARTS
+
+
+def load_scale_rows(queue, window, scales):
+    rows = scales[0].rearrange("(quad j) c -> j quad c", j=4)
+    for j in range(4):
+        queue.dma_start(out=window[j:P:32, :].bitcast(I32), in_=rows[j].bitcast(I32))
+
+
+def interleave_cast(nc, grouped, raw):
+    nc.scalar.copy(
+        out=grouped[:].rearrange("p (c i) t -> p c t i", i=4),
+        in_=raw[:].rearrange("p t (c i) -> p c t i", i=4),
+    )
+
+
+def tile_attend_lrgained_soft_kernel(
+    tc, query, keys_words, keys_scales, tab_words, tab_scales, w1, gain, slot_factor, value_scale, offs, out
+):
+    nc = tc.nc
+    with ExitStack() as ctx:
+        keep = ctx.enter_context(tc.tile_pool(name="keep", bufs=1))
+        psum = ctx.enter_context(tc.psum_pool(name="psum", bufs=1))
+
+        offsets = keep.tile([P, I // 16], U16, name="offsets")
+        kw_win = keep.tile([P, T], U16, name="kw_win", align_bytes=64)
+        ks_win = keep.tile([P, T], U8, name="ks_win", align_bytes=64)
+        tw_win = keep.tile([P, T], U16, name="tw_win", align_bytes=64)
+        ts_win = keep.tile([P, T], U8, name="ts_win", align_bytes=64)
+        q_raw = keep.tile([P, PACK, Q], F32, name="q_raw", tag="q_raw", align_bytes=64)
+        ident = keep.tile([P, P], F32, name="ident", align_bytes=64)
+        warm_in = keep.tile([P, 1], F32, name="warm_in", tag="w1_raw0", align_bytes=64)
+        warm_out = keep.tile([P, 1], F32, name="warm_out", tag="w1_raw1", align_bytes=64)
+
+        nc.vector.memset(ks_win[:].bitcast(I32), 0)
+        nc.gpsimd.memset(ts_win[:].bitcast(I32), 0)
+        nc.vector.memset(warm_in[:], 0.0)
+
+        nc.sync.dma_start(offsets[:], offs)
+        nc.sync.dma_start(out=kw_win[:].bitcast(I32), in_=keys_words[0].bitcast(I32))
+        load_scale_rows(nc.scalar, ks_win, keys_scales)
+        nc.scalar.activation(warm_out[:], warm_in[:], ACT.Exp)
+        nc.sync.dma_start(out=q_raw[:], in_=query.rearrange("(p t) q -> p t q", t=PACK))
+        nc.sync.dma_start(out=tw_win[:].bitcast(I32), in_=tab_words[0].bitcast(I32))
+        load_scale_rows(nc.gpsimd, ts_win, tab_scales)
+        make_identity(nc, ident[:])
+        w1_rows = w1.rearrange("(p t) r -> p t r", t=PACK)
+        w1_raw = [
+            keep.tile([P, PACK, W1_COLS], F32, name="w1_raw%d" % h, tag="w1_raw%d" % h, align_bytes=64)
+            for h in range(W1_PARTS)
+        ]
+        for h in range(W1_PARTS):
+            nc.sync.dma_start(out=w1_raw[h][:], in_=w1_rows[:, :, h * W1_COLS : (h + 1) * W1_COLS])
+
+        kw = keep.tile([P, I], U16, name="kw", align_bytes=64)
+        ks = keep.tile([P, I], U8, name="ks", align_bytes=64)
+        tw = keep.tile([P, I], U16, name="tw", align_bytes=64)
+        ts = keep.tile([P, I], U8, name="ts", align_bytes=64)
+        nc.vector.tensor_copy(ks[:], ks_win[:].indirect(offsets[:]))
+        nc.vector.tensor_copy(kw[:], kw_win[:].indirect(offsets[:]))
+
+        q_grouped = keep.tile([P, Q, PACK], BF16, name="q_grouped", align_bytes=64)
+        q_codes = keep.tile([P, Q], U32, name="q_codes", align_bytes=64)
+        q_scales = keep.tile([P, Q], U8, name="q_scales", align_bytes=64)
+        interleave_cast(nc, q_grouped, q_raw)
+        nc.vector.quantize_mx(
+            out=q_codes[:].bitcast(FP8X4), scales=q_scales[:], in_=q_grouped[:].rearrange("p q t -> p (q t)")
+        )
+        scores = psum.tile([P, I], F32, name="scores", tag="bank_c")
+        nc.tensor.matmul_mx(
+            out=scores[:], lhsT=q_codes[:].bitcast(FP8X4), lhsT_scale=q_scales[:],
+            rhs=kw[:].bitcast(FP4X4), rhs_scale=ks[:], start=True, stop=True,
+        )
+
+        nc.vector.tensor_copy(tw[:], tw_win[:].indirect(offsets[:]))
+        nc.vector.tensor_copy(ts[:], ts_win[:].indirect(offsets[:]))
+
+        rows = keep.tile([P, P], F32, name="rows", tag="q_raw", align_bytes=64)
+        nc.gpsimd.memset(rows[:], 0.0)
+        nc.sync.dma_start(out=rows[0:4, :], in_=slot_factor.rearrange("o (c n) -> (o c) n", n=P))
+        nc.sync.dma_start(out=rows[4:8, :], in_=value_scale.rearrange("o (c n) -> (o c) n", n=P))
+        nc.sync.dma_start(out=rows[8:12, :], in_=gain.rearrange("(c n) o -> c (n o)", n=P))
+        cols_ps = psum.tile([P, P], F32, name="cols_ps", tag="turn", bufs=2)
+        nc.tensor.transpose(cols_ps[:], rows[:], ident[:])
+        cols = keep.tile([P, 12], F32, name="cols")
+        nc.scalar.copy(out=cols[:], in_=cols_ps[:, 0:12])
+        os_row = psum.tile([P, I], F32, name="os_row", tag="bank_b")
+        vs_row = psum.tile([P, I], F32, name="vs_row", tag="bank_a")
+        for c in range(4):
+            nc.tensor.transpose(os_row[:, c * P : (c + 1) * P], cols[:, c : c + 1].to_broadcast([P, P]), ident[:])
+        for c in range(4):
+            nc.tensor.transpose(vs_row[:, c * P : (c + 1) * P], cols[:, 4 + c : 5 + c].to_broadcast([P, P]), ident[:])
+
+        w1_codes = []
+        w1_scales = []
+        for h in range(W1_PARTS):
+            grouped = keep.tile([P, W1_COLS, PACK], BF16, name="w1_grouped%d" % h, align_bytes=64)
+            codes = keep.tile([P, W1_COLS], U32, name="w1_codes%d" % h, align_bytes=64)
+            scales = keep.tile([P, W1_COLS], U8, name="w1_scales%d" % h, align_bytes=64)
+            interleave_cast(nc, grouped, w1_raw[h])
+            nc.vector.quantize_mx(
+                out=codes[:].bitcast(FP8X4), scales=scales[:], in_=grouped[:].rearrange("p r t -> p (r t)")
+            )
+            w1_codes.append(codes)
+            w1_scales.append(scales)
+
+        def turn_and_quantize(values, label):
+            words = values[:].bitcast(F32)
+            turned = psum.tile([P, 2, P], F32, name="turned" + label, tag="turn", bufs=2)
+            for u in range(2):
+                nc.tensor.transpose(turned[:, u, :], words[:, u : I // 2 : 2], ident[:])
+            grouped = keep.tile([P, P * PACK], BF16, name="grouped" + label, align_bytes=64)
+            nc.scalar.copy(
+                out=grouped[:].bitcast(F32).rearrange("p (n u) -> p n u", u=2),
+                in_=turned[:].rearrange("p u n -> p n u"),
+            )
+            codes = keep.tile([P, P], U32, name="codes" + label, align_bytes=64)
+            scales = keep.tile([P, P], U8, name="scales" + label, align_bytes=64)
+            nc.vector.quantize_mx(out=codes[:].bitcast(FP8X4), scales=scales[:], in_=grouped[:])
+            return codes, scales
+
+        neg_max = keep.tile([P, 1], F32, name="neg_max")
+        row_sum = keep.tile([P, 1], F32, name="row_sum")
+        inv_sum = keep.tile([P, 1], F32, name="inv_sum")
+        probs = keep.tile([P, I], F32, name="probs", align_bytes=64)
+        weights = keep.tile([P, I], BF16, name="weights", align_bytes=64)
+        nc.vector.tensor_reduce(neg_max[:], scores[:], mybir.AxisListType.X, ALU.max, negate=True)
+        nc.scalar.activation(probs[:], scores[:], ACT.Exp, bias=neg_max[:], accum_out=row_sum[:])
+        nc.vector.reciprocal(inv_sum[:], row_sum[:])
+        nc.vector.scalar_tensor_tensor(weights[:], probs[:], inv_sum[:], os_row[:], ALU.mult, ALU.mult)
+        w_codes, w_scales = turn_and_quantize(weights, "_w")
+
+        h_ops = []
+        for c in range(CHUNKS):
+            h, c0 = divmod(c * P, W1_COLS)
+            zh = psum.tile([P, I], F32, name="zh%d" % c, tag="zh", bufs=3)
+            nc.tensor.matmul_mx(
+                out=zh[:], lhsT=w1_codes[h][:, c0 : c0 + P].bitcast(FP8X4), lhsT_scale=w1_scales[h][:, c0 : c0 + P],
+                rhs=tw[:].bitcast(FP4X4), rhs_scale=ts[:], start=True, stop=True,
+            )
+            th = keep.tile([P, I], F32, name="th%d" % c, align_bytes=64)
+            nc.scalar.activation(th[:], zh[:], ACT.Tanh)
+            hb = keep.tile([P, I], BF16, name="hb%d" % c, align_bytes=64)
+            nc.vector.scalar_tensor_tensor(hb[:], th[:], cols[:, 8 + c : 9 + c], vs_row[:], ALU.mult, ALU.mult)
+            h_ops.append(turn_and_quantize(hb, "_h%d" % c))
+
+        for c in range(CHUNKS):
+            acc = psum.tile([P, P], F32, name="acc%d" % c, tag=("bank_c", "bank_b")[c % 2])
+            nc.tensor.matmul_mx(
+                out=acc[:], lhsT=w_codes[:].bitcast(FP8X4), lhsT_scale=w_scales[:],
+                rhs=h_ops[c][0][:].bitcast(FP8X4), rhs_scale=h_ops[c][1][:], start=True, stop=True,
+            )
+            result = keep.tile([P, P], F32, name="result%d" % c, align_bytes=64)
+            nc.scalar.copy(out=result[:], in_=acc[:])
+            nc.sync.dma_start(out=out[:, c * P : (c + 1) * P], in_=result[:])

@@ -19,22 +19,8 @@ ALU = mybir.AluOpType
 
 P = 128
 PACK = 4
-CHUNKS = R // P
-W1_PARTS = 2
-W1_COLS = R // W1_PARTS
-
-
-def load_scale_rows(queue, window, scales):
-    rows = scales[0].rearrange("(quad j) c -> j quad c", j=4)
-    for j in range(4):
-        queue.dma_start(out=window[j:P:32, :].bitcast(I32), in_=rows[j].bitcast(I32))
-
-
-def interleave_cast(nc, grouped, raw):
-    nc.scalar.copy(
-        out=grouped[:].rearrange("p (c i) t -> p c t i", i=4),
-        in_=raw[:].rearrange("p t (c i) -> p c t i", i=4),
-    )
+HALVES = 2
+HALF = R // HALVES
 
 
 def tile_attend_lrgained_soft_kernel(
@@ -43,136 +29,169 @@ def tile_attend_lrgained_soft_kernel(
     nc = tc.nc
     with ExitStack() as ctx:
         keep = ctx.enter_context(tc.tile_pool(name="keep", bufs=1))
+        reuse = ctx.enter_context(tc.tile_pool(name="reuse", bufs=1))
         psum = ctx.enter_context(tc.psum_pool(name="psum", bufs=1))
 
+        def sbuf(shape, dtype, name, tag=None):
+            return keep.tile(shape, dtype, name=name, tag=tag or name, align_bytes=64)
+
+        def placed(shape, dtype, name, offset):
+            return reuse.tile(shape, dtype, name=name, align_bytes=64, offset=offset)
+
+        def load_scale_rows(window, scales):
+            rows = scales[0].rearrange("(quad j) c -> j quad c", j=4)
+            for j in range(4):
+                nc.sync.dma_start(out=window[j:P:32, :].bitcast(I32), in_=rows[j].bitcast(I32))
+
+        def quantize(grouped, label, offset=None):
+            width = grouped.shape[1] // PACK
+            if offset is None:
+                codes = sbuf([P, width], U32, label + "_codes")
+            else:
+                codes = placed([P, width], U32, label + "_codes", offset)
+            scales = sbuf([P, width], U8, label + "_scales")
+            nc.vector.quantize_mx(out=codes[:].bitcast(FP8X4), scales=scales[:], in_=grouped)
+            return codes, scales
+
         offsets = keep.tile([P, I // 16], U16, name="offsets")
-        kw_win = keep.tile([P, T], U16, name="kw_win", align_bytes=64)
-        ks_win = keep.tile([P, T], U8, name="ks_win", align_bytes=64)
-        tw_win = keep.tile([P, T], U16, name="tw_win", align_bytes=64)
-        ts_win = keep.tile([P, T], U8, name="ts_win", align_bytes=64)
-        q_raw = keep.tile([P, PACK, Q], F32, name="q_raw", tag="q_raw", align_bytes=64)
-        ident = keep.tile([P, P], F32, name="ident", align_bytes=64)
-        warm_in = keep.tile([P, 1], F32, name="warm_in", tag="w1_raw0", align_bytes=64)
-        warm_out = keep.tile([P, 1], F32, name="warm_out", tag="w1_raw1", align_bytes=64)
+        kw_win = sbuf([P, T], U16, "kw_win")
+        ks_win = placed([P, T], U8, "ks_win", 4096)
+        tw_win = sbuf([P, T], U16, "tw_win")
+        ts_win = sbuf([P, T], U8, "ts_win")
+        q_raw = sbuf([P, PACK, Q], F32, "q_raw")
+        w1_raw = [sbuf([P, PACK, HALF], F32, "w1_raw0"), placed([P, PACK, HALF], F32, "w1_raw1", 0)]
+        os_cols = sbuf([P, PACK], F32, "os_cols")
+        vs_cols = sbuf([P, PACK], F32, "vs_cols")
+        gain_cols = sbuf([P, HALVES, 2], F32, "gain_cols")
+        ident = sbuf([P, P], F32, "ident")
+        warm_in = sbuf([P, 1], F32, "warm_in")
+        warm_out = sbuf([P, 1], F32, "warm_out")
 
+        nc.vector.memset(ts_win[:].bitcast(I32), 0)
         nc.vector.memset(ks_win[:].bitcast(I32), 0)
-        nc.gpsimd.memset(ts_win[:].bitcast(I32), 0)
-        nc.vector.memset(warm_in[:], 0.0)
-
-        nc.sync.dma_start(offsets[:], offs)
-        nc.sync.dma_start(out=kw_win[:].bitcast(I32), in_=keys_words[0].bitcast(I32))
-        load_scale_rows(nc.scalar, ks_win, keys_scales)
+        nc.gpsimd.memset(warm_in[:], 0.0)
         nc.scalar.activation(warm_out[:], warm_in[:], ACT.Exp)
-        nc.sync.dma_start(out=q_raw[:], in_=query.rearrange("(p t) q -> p t q", t=PACK))
-        nc.sync.dma_start(out=tw_win[:].bitcast(I32), in_=tab_words[0].bitcast(I32))
-        load_scale_rows(nc.gpsimd, ts_win, tab_scales)
         make_identity(nc, ident[:])
+
         w1_rows = w1.rearrange("(p t) r -> p t r", t=PACK)
-        w1_raw = [
-            keep.tile([P, PACK, W1_COLS], F32, name="w1_raw%d" % h, tag="w1_raw%d" % h, align_bytes=64)
-            for h in range(W1_PARTS)
-        ]
-        for h in range(W1_PARTS):
-            nc.sync.dma_start(out=w1_raw[h][:], in_=w1_rows[:, :, h * W1_COLS : (h + 1) * W1_COLS])
+        nc.sync.dma_start(offsets[:], offs)
+        nc.sync.dma_start(out=tw_win[:].bitcast(I32), in_=tab_words[0].bitcast(I32))
+        load_scale_rows(ts_win, tab_scales)
+        nc.sync.dma_start(out=vs_cols[:], in_=value_scale.rearrange("o (p c) -> (o p) c", c=PACK))
+        nc.sync.dma_start(out=w1_raw[0][:], in_=w1_rows[:, :, 0:HALF])
+        nc.sync.dma_start(out=kw_win[:].bitcast(I32), in_=keys_words[0].bitcast(I32))
+        nc.sync.dma_start(out=os_cols[:], in_=slot_factor.rearrange("o (p c) -> (o p) c", c=PACK))
+        nc.sync.dma_start(out=gain_cols[:], in_=gain.rearrange("(h p e) o -> p h (e o)", h=HALVES, e=2))
+        nc.sync.dma_start(out=q_raw[:], in_=query.rearrange("(p t) q -> p t q", t=PACK))
+        nc.sync.dma_start(out=w1_raw[1][:], in_=w1_rows[:, :, HALF:R])
+        load_scale_rows(ks_win, keys_scales)
 
-        kw = keep.tile([P, I], U16, name="kw", align_bytes=64)
-        ks = keep.tile([P, I], U8, name="ks", align_bytes=64)
-        tw = keep.tile([P, I], U16, name="tw", align_bytes=64)
-        ts = keep.tile([P, I], U8, name="ts", align_bytes=64)
-        nc.vector.tensor_copy(ks[:], ks_win[:].indirect(offsets[:]))
+        def cast_w1(h):
+            grouped = sbuf([P, HALF, PACK], BF16, "w1_grouped%d" % h)
+            nc.scalar.copy(
+                out=grouped[:].rearrange("p (e c m) t -> p c t m e", e=2, m=2),
+                in_=w1_raw[h][:].rearrange("p t (c m e) -> p c t m e", e=2, m=2),
+            )
+            return grouped[:].rearrange("p r t -> p (r t)")
+
+        def spread(cols, name, tag):
+            row = psum.tile([P, PACK, P], F32, name=name, tag=tag)
+            for c in range(PACK):
+                nc.tensor.transpose(row[:, c, :], cols[:, c : c + 1].to_broadcast([P, P]), ident[:])
+            return row[:].rearrange("p c n -> p n c")
+
+        def by_place(tile):
+            return tile[:].rearrange("p (n c) -> p n c", c=PACK)
+
+        def hidden_tanh(c, w1_ops):
+            codes, scales = w1_ops
+            cols = slice((c % 2) * P, (c % 2 + 1) * P)
+            zh = psum.tile([P, I], F32, name="zh%d" % c, tag="zh", bufs=3)
+            nc.tensor.matmul_mx(
+                out=zh[:], lhsT=codes[:, cols].bitcast(FP8X4), lhsT_scale=scales[:, cols],
+                rhs=tw[:].bitcast(FP4X4), rhs_scale=ts[:], start=True, stop=True,
+            )
+            th = placed([P, I], F32, "th%d" % c, 2048 * c) if c < 2 else sbuf([P, I], F32, "th%d" % c)
+            nc.scalar.activation(th[:], zh[:], ACT.Tanh)
+            return th
+
+        def hidden_scale(c, th):
+            hb = placed([P, I], BF16, "hb%d" % c, (5120, 1024)[c]) if c < 2 else sbuf([P, I], BF16, "hb%d" % c)
+            nc.vector.scalar_tensor_tensor(
+                by_place(hb), by_place(th), gain_cols[:, c // 2, c % 2 : c % 2 + 1], vs_slots, ALU.mult, ALU.mult
+            )
+            return hb
+
+        def turn(tiles, label):
+            count = len(tiles)
+            turned = psum.tile([P, count, 2, P], F32, name="turned_" + label, tag="turn", bufs=2)
+            for a, values in enumerate(tiles):
+                words = values[:].bitcast(F32)
+                for u in range(2):
+                    nc.tensor.transpose(turned[:, a, u, :], words[:, u : I // 2 : 2], ident[:])
+            grouped = sbuf([P, count * P * PACK], BF16, "grouped_" + label)
+            nc.scalar.copy(
+                out=grouped[:].bitcast(F32).rearrange("p (a n u) -> p a n u", a=count, u=2),
+                in_=turned[:].rearrange("p a u n -> p a n u"),
+            )
+            codes, scales = quantize(grouped[:], label)
+            return [(codes[:, a * P : (a + 1) * P], scales[:, a * P : (a + 1) * P]) for a in range(count)]
+
+        tw = sbuf([P, I], U16, "tw")
+        ts = sbuf([P, I], U8, "ts")
+        kw = sbuf([P, I], U16, "kw")
+        nc.vector.tensor_copy(tw[:], tw_win[:].indirect(offsets[:]))
+        nc.vector.tensor_copy(ts[:], ts_win[:].indirect(offsets[:]))
+        w1_grouped0 = cast_w1(0)
         nc.vector.tensor_copy(kw[:], kw_win[:].indirect(offsets[:]))
+        w1_ops0 = quantize(w1_grouped0, "w1_0")
+        vs_slots = spread(vs_cols, "vs_row", "bank_a")
+        os_slots = spread(os_cols, "os_row", "bank_b")
 
-        q_grouped = keep.tile([P, Q, PACK], BF16, name="q_grouped", align_bytes=64)
-        q_codes = keep.tile([P, Q], U32, name="q_codes", align_bytes=64)
-        q_scales = keep.tile([P, Q], U8, name="q_scales", align_bytes=64)
-        interleave_cast(nc, q_grouped, q_raw)
-        nc.vector.quantize_mx(
-            out=q_codes[:].bitcast(FP8X4), scales=q_scales[:], in_=q_grouped[:].rearrange("p q t -> p (q t)")
+        q_grouped = sbuf([P, Q, PACK], BF16, "q_grouped")
+        nc.scalar.copy(
+            out=q_grouped[:].rearrange("p (c i) t -> p c t i", i=4),
+            in_=q_raw[:].rearrange("p t (c i) -> p c t i", i=4),
         )
+        q_codes, q_scales = quantize(q_grouped[:].rearrange("p q t -> p (q t)"), "q")
+        ks = sbuf([P, I], U8, "ks", tag="q_grouped")
+        nc.vector.tensor_copy(ks[:], ks_win[:].indirect(offsets[:]))
+        w1_ops1 = quantize(cast_w1(1), "w1_1", 4096)
+        th0 = hidden_tanh(0, w1_ops0)
+        th1 = hidden_tanh(1, w1_ops0)
         scores = psum.tile([P, I], F32, name="scores", tag="bank_c")
         nc.tensor.matmul_mx(
             out=scores[:], lhsT=q_codes[:].bitcast(FP8X4), lhsT_scale=q_scales[:],
             rhs=kw[:].bitcast(FP4X4), rhs_scale=ks[:], start=True, stop=True,
         )
+        hb0 = hidden_scale(0, th0)
 
-        nc.vector.tensor_copy(tw[:], tw_win[:].indirect(offsets[:]))
-        nc.vector.tensor_copy(ts[:], ts_win[:].indirect(offsets[:]))
-
-        rows = keep.tile([P, P], F32, name="rows", tag="q_raw", align_bytes=64)
-        nc.gpsimd.memset(rows[:], 0.0)
-        nc.sync.dma_start(out=rows[0:4, :], in_=slot_factor.rearrange("o (c n) -> (o c) n", n=P))
-        nc.sync.dma_start(out=rows[4:8, :], in_=value_scale.rearrange("o (c n) -> (o c) n", n=P))
-        nc.sync.dma_start(out=rows[8:12, :], in_=gain.rearrange("(c n) o -> c (n o)", n=P))
-        cols_ps = psum.tile([P, P], F32, name="cols_ps", tag="turn", bufs=2)
-        nc.tensor.transpose(cols_ps[:], rows[:], ident[:])
-        cols = keep.tile([P, 12], F32, name="cols")
-        nc.scalar.copy(out=cols[:], in_=cols_ps[:, 0:12])
-        os_row = psum.tile([P, I], F32, name="os_row", tag="bank_b")
-        vs_row = psum.tile([P, I], F32, name="vs_row", tag="bank_a")
-        for c in range(4):
-            nc.tensor.transpose(os_row[:, c * P : (c + 1) * P], cols[:, c : c + 1].to_broadcast([P, P]), ident[:])
-        for c in range(4):
-            nc.tensor.transpose(vs_row[:, c * P : (c + 1) * P], cols[:, 4 + c : 5 + c].to_broadcast([P, P]), ident[:])
-
-        w1_codes = []
-        w1_scales = []
-        for h in range(W1_PARTS):
-            grouped = keep.tile([P, W1_COLS, PACK], BF16, name="w1_grouped%d" % h, align_bytes=64)
-            codes = keep.tile([P, W1_COLS], U32, name="w1_codes%d" % h, align_bytes=64)
-            scales = keep.tile([P, W1_COLS], U8, name="w1_scales%d" % h, align_bytes=64)
-            interleave_cast(nc, grouped, w1_raw[h])
-            nc.vector.quantize_mx(
-                out=codes[:].bitcast(FP8X4), scales=scales[:], in_=grouped[:].rearrange("p r t -> p (r t)")
-            )
-            w1_codes.append(codes)
-            w1_scales.append(scales)
-
-        def turn_and_quantize(values, label):
-            words = values[:].bitcast(F32)
-            turned = psum.tile([P, 2, P], F32, name="turned" + label, tag="turn", bufs=2)
-            for u in range(2):
-                nc.tensor.transpose(turned[:, u, :], words[:, u : I // 2 : 2], ident[:])
-            grouped = keep.tile([P, P * PACK], BF16, name="grouped" + label, align_bytes=64)
-            nc.scalar.copy(
-                out=grouped[:].bitcast(F32).rearrange("p (n u) -> p n u", u=2),
-                in_=turned[:].rearrange("p u n -> p n u"),
-            )
-            codes = keep.tile([P, P], U32, name="codes" + label, align_bytes=64)
-            scales = keep.tile([P, P], U8, name="scales" + label, align_bytes=64)
-            nc.vector.quantize_mx(out=codes[:].bitcast(FP8X4), scales=scales[:], in_=grouped[:])
-            return codes, scales
-
-        neg_max = keep.tile([P, 1], F32, name="neg_max")
-        row_sum = keep.tile([P, 1], F32, name="row_sum")
-        inv_sum = keep.tile([P, 1], F32, name="inv_sum")
-        probs = keep.tile([P, I], F32, name="probs", align_bytes=64)
-        weights = keep.tile([P, I], BF16, name="weights", align_bytes=64)
+        neg_max = placed([P, 1], F32, "neg_max", 0)
+        row_sum = sbuf([P, 1], F32, "row_sum")
+        inv_sum = sbuf([P, 1], F32, "inv_sum")
+        probs = sbuf([P, I], F32, "probs")
+        weights = sbuf([P, I], BF16, "weights")
         nc.vector.tensor_reduce(neg_max[:], scores[:], mybir.AxisListType.X, ALU.max, negate=True)
+        th2 = hidden_tanh(2, w1_ops1)
         nc.scalar.activation(probs[:], scores[:], ACT.Exp, bias=neg_max[:], accum_out=row_sum[:])
+        hb1 = hidden_scale(1, th1)
+        th3 = hidden_tanh(3, w1_ops1)
+        hb2 = hidden_scale(2, th2)
         nc.vector.reciprocal(inv_sum[:], row_sum[:])
-        nc.vector.scalar_tensor_tensor(weights[:], probs[:], inv_sum[:], os_row[:], ALU.mult, ALU.mult)
-        w_codes, w_scales = turn_and_quantize(weights, "_w")
+        nc.vector.scalar_tensor_tensor(by_place(weights), by_place(probs), inv_sum[:], os_slots, ALU.mult, ALU.mult)
+        hb3 = hidden_scale(3, th3)
+        h0_ops, h1_ops = turn([hb0, hb1], "h01")
+        h2_ops, (w_codes, w_scales) = turn([hb2, weights], "h2w")
+        h_ops = [h0_ops, h1_ops, h2_ops] + turn([hb3], "h3")
 
-        h_ops = []
-        for c in range(CHUNKS):
-            h, c0 = divmod(c * P, W1_COLS)
-            zh = psum.tile([P, I], F32, name="zh%d" % c, tag="zh", bufs=3)
-            nc.tensor.matmul_mx(
-                out=zh[:], lhsT=w1_codes[h][:, c0 : c0 + P].bitcast(FP8X4), lhsT_scale=w1_scales[h][:, c0 : c0 + P],
-                rhs=tw[:].bitcast(FP4X4), rhs_scale=ts[:], start=True, stop=True,
-            )
-            th = keep.tile([P, I], F32, name="th%d" % c, align_bytes=64)
-            nc.scalar.activation(th[:], zh[:], ACT.Tanh)
-            hb = keep.tile([P, I], BF16, name="hb%d" % c, align_bytes=64)
-            nc.vector.scalar_tensor_tensor(hb[:], th[:], cols[:, 8 + c : 9 + c], vs_row[:], ALU.mult, ALU.mult)
-            h_ops.append(turn_and_quantize(hb, "_h%d" % c))
-
-        for c in range(CHUNKS):
-            acc = psum.tile([P, P], F32, name="acc%d" % c, tag=("bank_c", "bank_b")[c % 2])
-            nc.tensor.matmul_mx(
-                out=acc[:], lhsT=w_codes[:].bitcast(FP8X4), lhsT_scale=w_scales[:],
-                rhs=h_ops[c][0][:].bitcast(FP8X4), rhs_scale=h_ops[c][1][:], start=True, stop=True,
-            )
-            result = keep.tile([P, P], F32, name="result%d" % c, align_bytes=64)
-            nc.scalar.copy(out=result[:], in_=acc[:])
-            nc.sync.dma_start(out=out[:, c * P : (c + 1) * P], in_=result[:])
+        for h in range(HALVES):
+            acc = psum.tile([P, 2, P], F32, name="acc%d" % h, tag=("bank_c", "bank_b")[h])
+            for e in range(2):
+                codes, scales = h_ops[2 * h + e]
+                nc.tensor.matmul_mx(
+                    out=acc[:, e, :], lhsT=w_codes.bitcast(FP8X4), lhsT_scale=w_scales,
+                    rhs=codes.bitcast(FP8X4), rhs_scale=scales, start=True, stop=True,
+                )
+            result = sbuf([P, P, 2], F32, "result%d" % h)
+            nc.scalar.copy(out=result[:], in_=acc[:].rearrange("p e n -> p n e"))
+            nc.sync.dma_start(out=out[:, h * HALF : (h + 1) * HALF], in_=result[:].rearrange("p n e -> p (n e)"))

@@ -55,36 +55,36 @@ def tile_attend_lrgained_soft_kernel(
 
         offsets = keep.tile([P, I // 16], U16, name="offsets")
         kw_win = sbuf([P, T], U16, "kw_win")
-        ks_win = placed([P, T], U8, "ks_win", 4096)
+        ks_win = sbuf([P, T], U8, "ks_win")
         tw_win = sbuf([P, T], U16, "tw_win")
-        ts_win = sbuf([P, T], U8, "ts_win")
+        ts_win = placed([P, T], U8, "ts_win", 4096)
         q_raw = sbuf([P, PACK, Q], F32, "q_raw")
         w1_raw = [sbuf([P, PACK, HALF], F32, "w1_raw0"), placed([P, PACK, HALF], F32, "w1_raw1", 0)]
-        os_cols = sbuf([P, PACK], F32, "os_cols")
-        vs_cols = sbuf([P, PACK], F32, "vs_cols")
+        rows = sbuf([P, P], F32, "rows")
         gain_cols = sbuf([P, HALVES, 2], F32, "gain_cols")
         ident = sbuf([P, P], F32, "ident")
         warm_in = sbuf([P, 1], F32, "warm_in")
         warm_out = sbuf([P, 1], F32, "warm_out")
 
-        nc.vector.memset(ts_win[:].bitcast(I32), 0)
         nc.vector.memset(ks_win[:].bitcast(I32), 0)
+        nc.vector.memset(ts_win[:].bitcast(I32), 0)
         nc.gpsimd.memset(warm_in[:], 0.0)
         nc.scalar.activation(warm_out[:], warm_in[:], ACT.Exp)
+        nc.gpsimd.memset(rows[:], 0.0)
         make_identity(nc, ident[:])
 
         w1_rows = w1.rearrange("(p t) r -> p t r", t=PACK)
         nc.sync.dma_start(offsets[:], offs)
-        nc.sync.dma_start(out=tw_win[:].bitcast(I32), in_=tab_words[0].bitcast(I32))
-        load_scale_rows(ts_win, tab_scales)
-        nc.sync.dma_start(out=vs_cols[:], in_=value_scale.rearrange("o (p c) -> (o p) c", c=PACK))
-        nc.sync.dma_start(out=w1_raw[0][:], in_=w1_rows[:, :, 0:HALF])
         nc.sync.dma_start(out=kw_win[:].bitcast(I32), in_=keys_words[0].bitcast(I32))
-        nc.sync.dma_start(out=os_cols[:], in_=slot_factor.rearrange("o (p c) -> (o p) c", c=PACK))
-        nc.sync.dma_start(out=gain_cols[:], in_=gain.rearrange("(h p e) o -> p h (e o)", h=HALVES, e=2))
-        nc.sync.dma_start(out=q_raw[:], in_=query.rearrange("(p t) q -> p t q", t=PACK))
-        nc.sync.dma_start(out=w1_raw[1][:], in_=w1_rows[:, :, HALF:R])
         load_scale_rows(ks_win, keys_scales)
+        nc.sync.dma_start(out=q_raw[:], in_=query.rearrange("(p t) q -> p t q", t=PACK))
+        nc.sync.dma_start(out=tw_win[:].bitcast(I32), in_=tab_words[0].bitcast(I32))
+        nc.sync.dma_start(out=rows[0:4, :], in_=slot_factor.rearrange("o (c n) -> (o c) n", n=P))
+        nc.sync.dma_start(out=rows[4:8, :], in_=value_scale.rearrange("o (c n) -> (o c) n", n=P))
+        nc.sync.dma_start(out=w1_raw[0][:], in_=w1_rows[:, :, 0:HALF])
+        load_scale_rows(ts_win, tab_scales)
+        nc.sync.dma_start(out=w1_raw[1][:], in_=w1_rows[:, :, HALF:R])
+        nc.sync.dma_start(out=gain_cols[:], in_=gain.rearrange("(h p e) o -> p h (e o)", h=HALVES, e=2))
 
         def cast_w1(h):
             grouped = sbuf([P, HALF, PACK], BF16, "w1_grouped%d" % h)
@@ -95,18 +95,15 @@ def tile_attend_lrgained_soft_kernel(
             return grouped[:].rearrange("p r t -> p (r t)")
 
         def spread(cols, name, tag):
-            row = psum.tile([P, PACK, P], F32, name=name, tag=tag)
-            for c in range(PACK):
-                nc.tensor.transpose(row[:, c, :], cols[:, c : c + 1].to_broadcast([P, P]), ident[:])
-            return row[:].rearrange("p c n -> p n c")
-
-        def by_place(tile):
-            return tile[:].rearrange("p (n c) -> p n c", c=PACK)
+            row = psum.tile([P, I], F32, name=name, tag=tag)
+            for c in range(I // P):
+                nc.tensor.transpose(row[:, c * P : (c + 1) * P], cols[:, c : c + 1].to_broadcast([P, P]), ident[:])
+            return row
 
         def hidden_tanh(c, w1_ops):
             codes, scales = w1_ops
             cols = slice((c % 2) * P, (c % 2 + 1) * P)
-            zh = psum.tile([P, I], F32, name="zh%d" % c, tag="zh", bufs=3)
+            zh = psum.tile([P, I], F32, name="zh%d" % c, tag="zh%d" % c)
             nc.tensor.matmul_mx(
                 out=zh[:], lhsT=codes[:, cols].bitcast(FP8X4), lhsT_scale=scales[:, cols],
                 rhs=tw[:].bitcast(FP4X4), rhs_scale=ts[:], start=True, stop=True,
@@ -116,15 +113,15 @@ def tile_attend_lrgained_soft_kernel(
             return th
 
         def hidden_scale(c, th):
-            hb = placed([P, I], BF16, "hb%d" % c, (5120, 1024)[c]) if c < 2 else sbuf([P, I], BF16, "hb%d" % c)
+            hb = sbuf([P, I], BF16, "hb%d" % c)
             nc.vector.scalar_tensor_tensor(
-                by_place(hb), by_place(th), gain_cols[:, c // 2, c % 2 : c % 2 + 1], vs_slots, ALU.mult, ALU.mult
+                hb[:], th[:], gain_cols[:, c // 2, c % 2 : c % 2 + 1], vs_row[:], ALU.mult, ALU.mult
             )
             return hb
 
-        def turn(tiles, label):
+        def turn(tiles, label, bank):
             count = len(tiles)
-            turned = psum.tile([P, count, 2, P], F32, name="turned_" + label, tag="turn", bufs=2)
+            turned = psum.tile([P, count, 2, P], F32, name="turned_" + label, tag=bank)
             for a, values in enumerate(tiles):
                 words = values[:].bitcast(F32)
                 for u in range(2):
@@ -140,49 +137,47 @@ def tile_attend_lrgained_soft_kernel(
         tw = sbuf([P, I], U16, "tw")
         ts = sbuf([P, I], U8, "ts")
         kw = sbuf([P, I], U16, "kw")
-        nc.vector.tensor_copy(tw[:], tw_win[:].indirect(offsets[:]))
-        nc.vector.tensor_copy(ts[:], ts_win[:].indirect(offsets[:]))
-        w1_grouped0 = cast_w1(0)
+        ks = sbuf([P, I], U8, "ks")
         nc.vector.tensor_copy(kw[:], kw_win[:].indirect(offsets[:]))
-        w1_ops0 = quantize(w1_grouped0, "w1_0")
-        vs_slots = spread(vs_cols, "vs_row", "bank_a")
-        os_slots = spread(os_cols, "os_row", "bank_b")
-
+        nc.vector.tensor_copy(ks[:], ks_win[:].indirect(offsets[:]))
         q_grouped = sbuf([P, Q, PACK], BF16, "q_grouped")
         nc.scalar.copy(
             out=q_grouped[:].rearrange("p (c i) t -> p c t i", i=4),
             in_=q_raw[:].rearrange("p t (c i) -> p c t i", i=4),
         )
         q_codes, q_scales = quantize(q_grouped[:].rearrange("p q t -> p (q t)"), "q")
-        ks = sbuf([P, I], U8, "ks", tag="q_grouped")
-        nc.vector.tensor_copy(ks[:], ks_win[:].indirect(offsets[:]))
-        w1_ops1 = quantize(cast_w1(1), "w1_1", 4096)
-        th0 = hidden_tanh(0, w1_ops0)
-        th1 = hidden_tanh(1, w1_ops0)
         scores = psum.tile([P, I], F32, name="scores", tag="bank_c")
         nc.tensor.matmul_mx(
             out=scores[:], lhsT=q_codes[:].bitcast(FP8X4), lhsT_scale=q_scales[:],
             rhs=kw[:].bitcast(FP4X4), rhs_scale=ks[:], start=True, stop=True,
         )
-        hb0 = hidden_scale(0, th0)
-
-        neg_max = placed([P, 1], F32, "neg_max", 0)
-        row_sum = sbuf([P, 1], F32, "row_sum")
-        inv_sum = sbuf([P, 1], F32, "inv_sum")
-        probs = sbuf([P, I], F32, "probs")
-        weights = sbuf([P, I], BF16, "weights")
+        nc.vector.tensor_copy(tw[:], tw_win[:].indirect(offsets[:]))
+        neg_max = sbuf([P, 1], F32, "neg_max", tag="tw_win")
         nc.vector.tensor_reduce(neg_max[:], scores[:], mybir.AxisListType.X, ALU.max, negate=True)
-        th2 = hidden_tanh(2, w1_ops1)
+        nc.vector.tensor_copy(ts[:], ts_win[:].indirect(offsets[:]))
+
+        cols_turned = psum.tile([P, P], F32, name="cols_turned", tag="zh0")
+        nc.tensor.transpose(cols_turned[:], rows[:], ident[:])
+        cols = sbuf([P, 8], F32, "cols")
+        nc.scalar.copy(out=cols[:], in_=cols_turned[:, 0:8])
+        os_row = spread(cols[:, 0:4], "os_row", "bank_b")
+        vs_row = spread(cols[:, 4:8], "vs_row", "bank_a")
+
+        w1_ops0 = quantize(cast_w1(0), "w1_0", 4096)
+        row_sum = sbuf([P, 1], F32, "row_sum")
+        inv_sum = placed([P, 1], F32, "inv_sum", 5120)
+        probs = sbuf([P, I], F32, "probs", tag="w1_raw0")
+        weights = sbuf([P, I], BF16, "weights")
         nc.scalar.activation(probs[:], scores[:], ACT.Exp, bias=neg_max[:], accum_out=row_sum[:])
-        hb1 = hidden_scale(1, th1)
-        th3 = hidden_tanh(3, w1_ops1)
-        hb2 = hidden_scale(2, th2)
+        w1_grouped1 = cast_w1(1)
         nc.vector.reciprocal(inv_sum[:], row_sum[:])
-        nc.vector.scalar_tensor_tensor(by_place(weights), by_place(probs), inv_sum[:], os_slots, ALU.mult, ALU.mult)
-        hb3 = hidden_scale(3, th3)
-        h0_ops, h1_ops = turn([hb0, hb1], "h01")
-        h2_ops, (w_codes, w_scales) = turn([hb2, weights], "h2w")
-        h_ops = [h0_ops, h1_ops, h2_ops] + turn([hb3], "h3")
+        nc.vector.scalar_tensor_tensor(weights[:], probs[:], inv_sum[:], os_row[:], ALU.mult, ALU.mult)
+        w1_ops1 = quantize(w1_grouped1, "w1_1")
+
+        tanhs = [hidden_tanh(c, (w1_ops0, w1_ops1)[c // 2]) for c in range(4)]
+        hbs = [hidden_scale(c, tanhs[c]) for c in range(4)]
+        (w_codes, w_scales), h0_ops = turn([weights, hbs[0]], "wh0", "zh2")
+        h_ops = [h0_ops] + turn(hbs[1:2], "h1", "zh3") + turn(hbs[2:3], "h2", "zh0") + turn(hbs[3:4], "h3", "zh1")
 
         for h in range(HALVES):
             acc = psum.tile([P, 2, P], F32, name="acc%d" % h, tag=("bank_c", "bank_b")[h])
@@ -193,5 +188,5 @@ def tile_attend_lrgained_soft_kernel(
                     rhs=codes.bitcast(FP8X4), rhs_scale=scales, start=True, stop=True,
                 )
             result = sbuf([P, P, 2], F32, "result%d" % h)
-            nc.scalar.copy(out=result[:], in_=acc[:].rearrange("p e n -> p n e"))
+            (nc.scalar.copy, nc.vector.tensor_copy)[h](out=result[:], in_=acc[:].rearrange("p e n -> p n e"))
             nc.sync.dma_start(out=out[:, h * HALF : (h + 1) * HALF], in_=result[:].rearrange("p n e -> p (n e)"))

from contextlib import ExitStack

import concourse.mybir as mybir
from concourse.masks import make_identity

D, K, R, T, I, Q = 512, 512, 512, 2048, 512, 128
FLOPS = 2 * (D * Q * I + K * R * I + I * Q * R)

F32 = mybir.dt.float32
BF16 = mybir.dt.bfloat16
I32 = mybir.dt.int32
U32 = mybir.dt.uint32
U16 = mybir.dt.uint16
U8 = mybir.dt.uint8
FP8X4 = mybir.dt.float8_e4m3fn_x4
FP4X4 = mybir.dt.float4_e2m1fn_x4
ACT = mybir.ActivationFunctionType
ALU = mybir.AluOpType

P = 128
PACK = 4
HALVES = 2
HALF = R // HALVES


def tile_attend_lrgained_soft_kernel(
    tc, query, keys_words, keys_scales, tab_words, tab_scales, w1, gain, slot_factor, value_scale, offs, out
):
    nc = tc.nc
    with ExitStack() as ctx:
        keep = ctx.enter_context(tc.tile_pool(name="keep", bufs=1))
        reuse = ctx.enter_context(tc.tile_pool(name="reuse", bufs=1))
        psum = ctx.enter_context(tc.psum_pool(name="psum", bufs=1))

        def sbuf(shape, dtype, name, tag=None):
            return keep.tile(shape, dtype, name=name, tag=tag or name, align_bytes=64)

        def placed(shape, dtype, name, offset):
            return reuse.tile(shape, dtype, name=name, align_bytes=64, offset=offset)

        def load_scale_rows(window, scales):
            rows = scales[0].rearrange("(quad j) c -> j quad c", j=4)
            for j in range(4):
                nc.sync.dma_start(out=window[j:P:32, :].bitcast(I32), in_=rows[j].bitcast(I32))

        def quantize(grouped, label, offset=None):
            width = grouped.shape[1] // PACK
            if offset is None:
                codes = sbuf([P, width], U32, label + "_codes")
            else:
                codes = placed([P, width], U32, label + "_codes", offset)
            scales = sbuf([P, width], U8, label + "_scales")
            nc.vector.quantize_mx(out=codes[:].bitcast(FP8X4), scales=scales[:], in_=grouped)
            return codes, scales

        offsets = keep.tile([P, I // 16], U16, name="offsets")
        kw_win = sbuf([P, T], U16, "kw_win")
        ks_win = sbuf([P, T], U8, "ks_win")
        tw_win = sbuf([P, T], U16, "tw_win")
        ts_win = placed([P, T], U8, "ts_win", 4096)
        q_raw = sbuf([P, PACK, Q], F32, "q_raw")
        w1_raw = [sbuf([P, PACK, HALF], F32, "w1_raw0"), placed([P, PACK, HALF], F32, "w1_raw1", 0)]
        rows = sbuf([P, P], F32, "rows")
        gain_cols = sbuf([P, HALVES, 2], F32, "gain_cols")
        ident = sbuf([P, P], F32, "ident")
        warm_in = sbuf([P, 1], F32, "warm_in")
        warm_out = sbuf([P, 1], F32, "warm_out")

        nc.vector.memset(ks_win[:].bitcast(I32), 0)
        nc.vector.memset(ts_win[:].bitcast(I32), 0)
        nc.gpsimd.memset(warm_in[:], 0.0)
        nc.scalar.activation(warm_out[:], warm_in[:], ACT.Exp)
        nc.gpsimd.memset(rows[:], 0.0)
        make_identity(nc, ident[:])

        w1_rows = w1.rearrange("(p t) r -> p t r", t=PACK)
        nc.sync.dma_start(offsets[:], offs)
        nc.sync.dma_start(out=kw_win[:].bitcast(I32), in_=keys_words[0].bitcast(I32))
        load_scale_rows(ks_win, keys_scales)
        nc.sync.dma_start(out=q_raw[:], in_=query.rearrange("(p t) q -> p t q", t=PACK))
        nc.sync.dma_start(out=tw_win[:].bitcast(I32), in_=tab_words[0].bitcast(I32))
        nc.sync.dma_start(out=rows[0:4, :], in_=slot_factor.rearrange("o (c n) -> (o c) n", n=P))
        nc.sync.dma_start(out=rows[4:8, :], in_=value_scale.rearrange("o (c n) -> (o c) n", n=P))
        nc.sync.dma_start(out=w1_raw[0][:], in_=w1_rows[:, :, 0:HALF])
        load_scale_rows(ts_win, tab_scales)
        nc.sync.dma_start(out=w1_raw[1][:], in_=w1_rows[:, :, HALF:R])
        nc.sync.dma_start(out=gain_cols[:], in_=gain.rearrange("(h p e) o -> p h (e o)", h=HALVES, e=2))

        def cast_w1(h):
            grouped = sbuf([P, HALF, PACK], BF16, "w1_grouped%d" % h)
            nc.scalar.copy(
                out=grouped[:].rearrange("p (e c m) t -> p c t m e", e=2, m=2),
                in_=w1_raw[h][:].rearrange("p t (c m e) -> p c t m e", e=2, m=2),
            )
            return grouped[:].rearrange("p r t -> p (r t)")

        def spread(cols, name, tag):
            row = psum.tile([P, I], F32, name=name, tag=tag)
            for c in range(I // P):
                nc.tensor.transpose(row[:, c * P : (c + 1) * P], cols[:, c : c + 1].to_broadcast([P, P]), ident[:])
            return row

        def hidden_tanh(c, w1_ops):
            codes, scales = w1_ops
            cols = slice((c % 2) * P, (c % 2 + 1) * P)
            zh = psum.tile([P, I], F32, name="zh%d" % c, tag="zh%d" % c)
            nc.tensor.matmul_mx(
                out=zh[:], lhsT=codes[:, cols].bitcast(FP8X4), lhsT_scale=scales[:, cols],
                rhs=tw[:].bitcast(FP4X4), rhs_scale=ts[:], start=True, stop=True,
            )
            th = placed([P, I], F32, "th%d" % c, 2048 * c) if c < 2 else sbuf([P, I], F32, "th%d" % c)
            nc.scalar.activation(th[:], zh[:], ACT.Tanh)
            return th

        def hidden_scale(c, th):
            hb = sbuf([P, I], BF16, "hb%d" % c)
            nc.vector.scalar_tensor_tensor(
                hb[:], th[:], gain_cols[:, c // 2, c % 2 : c % 2 + 1], vs_row[:], ALU.mult, ALU.mult
            )
            return hb

        def turn(tiles, label, bank):
            count = len(tiles)
            turned = psum.tile([P, count, 2, P], F32, name="turned_" + label, tag=bank)
            for a, values in enumerate(tiles):
                words = values[:].bitcast(F32)
                for u in range(2):
                    nc.tensor.transpose(turned[:, a, u, :], words[:, u : I // 2 : 2], ident[:])
            grouped = sbuf([P, count * P * PACK], BF16, "grouped_" + label)
            nc.scalar.copy(
                out=grouped[:].bitcast(F32).rearrange("p (a n u) -> p a n u", a=count, u=2),
                in_=turned[:].rearrange("p a u n -> p a n u"),
            )
            codes, scales = quantize(grouped[:], label)
            return [(codes[:, a * P : (a + 1) * P], scales[:, a * P : (a + 1) * P]) for a in range(count)]

        tw = sbuf([P, I], U16, "tw")
        ts = sbuf([P, I], U8, "ts")
        kw = sbuf([P, I], U16, "kw")
        ks = sbuf([P, I], U8, "ks")
        nc.vector.tensor_copy(kw[:], kw_win[:].indirect(offsets[:]))
        nc.vector.tensor_copy(ks[:], ks_win[:].indirect(offsets[:]))
        q_grouped = sbuf([P, Q, PACK], BF16, "q_grouped")
        nc.scalar.copy(
            out=q_grouped[:].rearrange("p (c i) t -> p c t i", i=4),
            in_=q_raw[:].rearrange("p t (c i) -> p c t i", i=4),
        )
        q_codes, q_scales = quantize(q_grouped[:].rearrange("p q t -> p (q t)"), "q")
        scores = psum.tile([P, I], F32, name="scores", tag="bank_c")
        nc.tensor.matmul_mx(
            out=scores[:], lhsT=q_codes[:].bitcast(FP8X4), lhsT_scale=q_scales[:],
            rhs=kw[:].bitcast(FP4X4), rhs_scale=ks[:], start=True, stop=True,
        )
        nc.vector.tensor_copy(tw[:], tw_win[:].indirect(offsets[:]))
        neg_max = sbuf([P, 1], F32, "neg_max", tag="tw_win")
        nc.vector.tensor_reduce(neg_max[:], scores[:], mybir.AxisListType.X, ALU.max, negate=True)
        nc.vector.tensor_copy(ts[:], ts_win[:].indirect(offsets[:]))

        cols_turned = psum.tile([P, P], F32, name="cols_turned", tag="zh0")
        nc.tensor.transpose(cols_turned[:], rows[:], ident[:])
        cols = sbuf([P, 8], F32, "cols")
        nc.scalar.copy(out=cols[:], in_=cols_turned[:, 0:8])
        os_row = spread(cols[:, 0:4], "os_row", "bank_b")
        vs_row = spread(cols[:, 4:8], "vs_row", "bank_a")

        w1_ops0 = quantize(cast_w1(0), "w1_0", 4096)
        row_sum = sbuf([P, 1], F32, "row_sum")
        inv_sum = placed([P, 1], F32, "inv_sum", 5120)
        probs = sbuf([P, I], F32, "probs", tag="w1_raw0")
        weights = sbuf([P, I], BF16, "weights")
        nc.scalar.activation(probs[:], scores[:], ACT.Exp, bias=neg_max[:], accum_out=row_sum[:])
        w1_grouped1 = cast_w1(1)
        nc.vector.reciprocal(inv_sum[:], row_sum[:])
        nc.vector.scalar_tensor_tensor(weights[:], probs[:], inv_sum[:], os_row[:], ALU.mult, ALU.mult)
        w1_ops1 = quantize(w1_grouped1, "w1_1")

        tanhs = [hidden_tanh(c, (w1_ops0, w1_ops1)[c // 2]) for c in range(4)]
        hbs = [hidden_scale(c, tanhs[c]) for c in range(4)]
        (w_codes, w_scales), h0_ops = turn([weights, hbs[0]], "wh0", "zh2")
        h_ops = [h0_ops] + turn(hbs[1:2], "h1", "zh3") + turn(hbs[2:3], "h2", "zh0") + turn(hbs[3:4], "h3", "zh1")

        for h in range(HALVES):
            acc = psum.tile([P, 2, P], F32, name="acc%d" % h, tag=("bank_c", "bank_b")[h])
            for e in range(2):
                codes, scales = h_ops[2 * h + e]
                nc.tensor.matmul_mx(
                    out=acc[:, e, :], lhsT=w_codes.bitcast(FP8X4), lhsT_scale=w_scales,
                    rhs=codes.bitcast(FP8X4), rhs_scale=scales, start=True, stop=True,
                )
            result = sbuf([P, P, 2], F32, "result%d" % h)
            (nc.scalar.copy, nc.vector.tensor_copy)[h](out=result[:], in_=acc[:].rearrange("p e n -> p n e"))
            nc.sync.dma_start(out=out[:, h * HALF : (h + 1) * HALF], in_=result[:].rearrange("p n e -> p (n e)"))
